import numpy as np
import ml_dtypes


def mxq(x, axis, fmt="e4m3"):
    dtype, down = {"e4m3": (ml_dtypes.float8_e4m3fn, 7), "e5m2": (ml_dtypes.float8_e5m2, 14)}[fmt]
    v = np.moveaxis(np.asarray(x, np.float32).astype(ml_dtypes.bfloat16).astype(np.float64), axis, -1)
    blocks = v.reshape(v.shape[:-1] + (-1, 32))
    amax = np.abs(blocks).max(-1, keepdims=True)
    byte = np.maximum(np.where(amax > 0, np.frexp(amax)[1] - 1 + 127, 0) - down, 1)
    scale = np.exp2(byte - 127.0)
    codes = (blocks / scale).astype(np.float32).astype(dtype).astype(np.float64)
    return np.moveaxis((codes * scale).reshape(v.shape), -1, axis)


WIDE = False


def mx_kscale(k):
    if not WIDE:
        return np.ones(k)
    levels = np.array([10, -10, 5, -5, 0])
    if k % 512:
        return np.exp2(np.random.permutation(np.resize(levels, k // 32))).repeat(32)
    a = np.empty((k // 512, 16))
    for p in range(k // 512):
        a[p, :8] = np.random.permutation(np.resize(levels, 8))
        for g in range(8):
            far = levels[np.abs(levels - a[p, g]) >= 10]
            a[p, g + 8] = far[np.random.randint(len(far))]
    return np.exp2(a.ravel()).repeat(32)


def f64(x):
    return np.asarray(x).astype(np.float64)


def striped(idx):
    return np.tile(idx.reshape(-1, 16).T, (8, 1)).astype(np.uint16)


def unstriped(offs):
    return offs[:16].T.reshape(-1).astype(np.int64)


E2M1 = np.array([0.0, 0.5, 1.0, 1.5, 2.0, 3.0, 4.0, 6.0, -0.0, -0.5, -1.0, -1.5, -2.0, -3.0, -4.0, -6.0])


def pack_weight(w, fmt):
    k, n = w.shape
    w = f64(np.asarray(w, np.float32).astype(ml_dtypes.bfloat16)).reshape(k // 32, 32, n)
    amax = np.abs(w).max(1)
    if fmt == "e4m3":
        byte = np.frexp(amax)[1] - 1 + 127 - 7
    else:
        mant, ex = np.frexp(amax / 6.0)
        byte = np.where(mant > 0.5, ex, ex - 1) + 127
    byte = np.clip(np.where(amax > 0, byte, 1), 1, 254)
    scaled = (w * np.exp2(127.0 - byte)[:, None, :]).reshape(k, n).astype(np.float32)
    by_word = np.ascontiguousarray(scaled.reshape(k // 512, 128, 4, n).transpose(0, 1, 3, 2))
    if fmt == "e4m3":
        words = by_word.astype(ml_dtypes.float8_e4m3fn).view(np.uint8)
    else:
        c = by_word.astype(ml_dtypes.float4_e2m1fn).view(np.uint8) & 0xF
        words = (c[..., 0::2] | (c[..., 1::2] << 4)).reshape(k // 512, 128, 2 * n)
    return np.ascontiguousarray(words), np.ascontiguousarray(byte.astype(np.uint8).reshape(k // 512, 16, n))


def unpack_weight(words, scales, fmt):
    g, _, n = scales.shape
    words = np.ascontiguousarray(words).reshape(g, 128, n, -1)
    if fmt == "e4m3":
        vals = words.view(ml_dtypes.float8_e4m3fn).astype(np.float64)
    else:
        nib = np.empty((g, 128, n, 4), np.uint8)
        nib[..., 0::2] = words & 0xF
        nib[..., 1::2] = words >> 4
        vals = E2M1[nib]
    vals = vals * np.repeat(np.exp2(scales.astype(np.float64) - 127.0), 8, axis=1)[..., None]
    return vals.transpose(0, 1, 3, 2).reshape(g * 512, n)


def relu2(v):
    return np.maximum(v, 0.0) ** 2


K, T, E, C, D, H, N = 512, 1024, 4, 256, 128, 512, 512


def by_expert(wq, xq, C):
    return np.concatenate([wq[e].T @ xq[:, e * C:(e + 1) * C] for e in range(E)], axis=1)


def setup_inputs():
    n = np.random.standard_normal
    s = mx_kscale(K)
    u = mx_kscale(H)
    first = np.random.permutation(np.repeat(np.arange(E), C))
    slots1 = np.concatenate([np.random.permutation(np.flatnonzero(first == e)) for e in range(E)])
    free = np.ones(T, bool); slots2 = np.empty(E * D, np.int64)
    for e in np.random.permutation(E):
        pick = np.random.permutation(np.flatnonzero(free & (first != e)))[:D]; slots2[e * D:(e + 1) * D] = pick; free[pick] = False
    g1 = np.random.uniform(0.5, 1.0, T); g2 = 1.0 - g1
    x = pack_weight(n((K, T)) * s[:, None], "e4m3")
    w1 = [pack_weight(m, "e2m1") for m in n((E, K, H)) / np.sqrt(K) / s[None, :, None] * u]
    w2 = [pack_weight(m, "e2m1") for m in n((E, H, N)) / np.sqrt(H) / u[None, :, None] ** 2]
    return {
        "x_words": x[0],
        "x_scales": x[1],
        "w1_words": np.stack([m[0] for m in w1]),
        "w1_scales": np.stack([m[1] for m in w1]),
        "w2_words": np.stack([m[0] for m in w2]),
        "w2_scales": np.stack([m[1] for m in w2]),
        "gate1": (np.tile(g1[slots1], (128, 1))).astype(np.float32),
        "gate2": (np.tile(g2[slots2], (128, 1))).astype(np.float32),
        "offs": striped(slots1),
        "offs2": striped(slots2),
    }


def reference(x_words, x_scales, w1_words, w1_scales, w2_words, w2_scales, gate1, gate2, offs, offs2):
    w1 = np.stack([unpack_weight(w1_words[e], w1_scales[e], "e2m1") for e in range(E)])
    w2 = np.stack([unpack_weight(w2_words[e], w2_scales[e], "e2m1") for e in range(E)])
    idx, idx2 = unstriped(offs), unstriped(offs2)
    x = unpack_weight(x_words, x_scales, "e4m3")
    h = relu2(by_expert(w1, x[:, idx], C))
    y = by_expert(w2, mxq(h, 0, "e4m3"), C)
    h = relu2(by_expert(w1, x[:, idx2], D))
    z = by_expert(w2, mxq(h, 0, "e4m3"), D)
    out = np.zeros((N, T))
    out[:, idx] = f64(gate1[:1]) * y
    out[:, idx2] += f64(gate2[:1]) * z
    return out

@@ -1,0 +1,232 @@
+from contextlib import ExitStack
+
+import concourse.mybir as mybir
+from concourse.masks import make_identity
+
+K, T, E, C, D, H, N = 512, 1024, 4, 256, 128, 512, 512
+FLOPS = 2 * (E * C + E * D) * (K * H + H * N)
+
+F32 = mybir.dt.float32
+BF16 = mybir.dt.bfloat16
+I32 = mybir.dt.int32
+U32 = mybir.dt.uint32
+U16 = mybir.dt.uint16
+U8 = mybir.dt.uint8
+FP8X4 = mybir.dt.float8_e4m3fn_x4
+FP4X4 = mybir.dt.float4_e2m1fn_x4
+ACT = mybir.ActivationFunctionType
+ALU = mybir.AluOpType
+
+P = 128
+G = 256
+RB = N // P
+
+
+def tile_moe_ada_mlp_relu2_kernel(
+    tc, x_words, x_scales, w1_words, w1_scales, w2_words, w2_scales, gate1, gate2, offs, offs2, out
+):
+    nc = tc.nc
+    with ExitStack() as ctx:
+        lists = ctx.enter_context(tc.tile_pool(name="lists", bufs=1))
+        keep = ctx.enter_context(tc.tile_pool(name="keep", bufs=1))
+        ring = ctx.enter_context(tc.tile_pool(name="ring", bufs=3))
+        psum = ctx.enter_context(tc.psum_pool(name="psum", bufs=2))
+
+        list1 = lists.tile([P, E * C // 16], U16, name="list1")
+        list2 = lists.tile([P, E * D // 16], U16, name="list2")
+        xw = keep.tile([P, T], I32, name="xw", align_bytes=64)
+        xs = keep.tile([P, T], U8, name="xs", align_bytes=64)
+        w1s = keep.tile([P, E, H], U8, name="w1s", align_bytes=64)
+        w2s = keep.tile([P, E, N], U8, name="w2s", align_bytes=64)
+        w1_head = keep.tile([P, 2 * H], U8, name="w1_head", align_bytes=64)
+        ident = keep.tile([P, P], F32, name="ident", align_bytes=64)
+        first = [keep.tile([P, T], F32, name="first_%d" % r, align_bytes=64) for r in range(RB)]
+        second = [keep.tile([P, T], F32, name="second_%d" % i, align_bytes=64) for i in range(2)]
+
+        nc.vector.memset(xs[:].bitcast(I32), 0)
+        nc.vector.memset(w1s[:].bitcast(I32), 0)
+        nc.vector.memset(w2s[:].bitcast(I32), 0)
+        with tc.tile_pool(name="scratch", bufs=1) as scratch:
+            eye = scratch.tile([P, P], F32, name="eye", align_bytes=64)
+            make_identity(nc, eye[:])
+            nc.scalar.activation(ident[:], eye[:], ACT.Copy)
+        nc.vector.memset(second[0][:], 0.0)
+        nc.gpsimd.memset(second[1][:], 0.0)
+        late = ctx.enter_context(tc.tile_pool(name="late", bufs=1))
+        w1_rest = late.tile([P, 3, 2 * H], U8, name="w1_rest", align_bytes=64)
+        w2_head = late.tile([P, 2 * N], U8, name="w2_head", align_bytes=64)
+        w2_rest = late.tile([P, 3, 2 * N], U8, name="w2_rest", align_bytes=64)
+        gates = [late.tile([P, 2 * G], F32, name="gate_%d" % i, align_bytes=64) for i in range(3)]
+        w1 = [w1_head[:]] + [w1_rest[:, e, :] for e in range(3)]
+        w2 = [w2_head[:]] + [w2_rest[:, e, :] for e in range(3)]
+
+        def load_scales(plane, rows):
+            for r in range(4):
+                nc.sync.dma_start(out=plane[r:P:32], in_=rows[r])
+
+        def load_words(tile, words, a, b):
+            nc.sync.dma_start(
+                out=tile[:].bitcast(I32),
+                in_=words[a:b].rearrange("e s p b -> p (e s) b").bitcast(I32),
+            )
+
+        nc.sync.dma_start(list1[:], offs)
+        nc.sync.dma_start(out=xw[:], in_=x_words.rearrange("s p t d -> p (s t d)").bitcast(I32))
+        nc.sync.dma_start(out=w1_head[:].bitcast(I32), in_=w1_words[0, 0].bitcast(I32))
+        nc.sync.dma_start(list2[:], offs2)
+        load_scales(xs[:].bitcast(I32), x_scales.rearrange("s (q r) t -> r q (s t)", r=4).bitcast(I32))
+        load_scales(w1s[:].bitcast(I32), w1_scales.rearrange("e s (q r) i -> r q (e s) i", r=4).bitcast(I32))
+        load_words(w1_rest, w1_words, 1, 4)
+        load_scales(w2s[:].bitcast(I32), w2_scales.rearrange("e s (q r) i -> r q (e s) i", r=4).bitcast(I32))
+        nc.sync.dma_start(out=w2_head[:].bitcast(I32), in_=w2_words[0, 0].bitcast(I32))
+        nc.sync.dma_start(out=gates[0][:], in_=gate1[:, 0 : 2 * G])
+        load_words(w2_rest, w2_words, 1, 4)
+        nc.sync.dma_start(out=gates[1][:], in_=gate1[:, 2 * G : 4 * G])
+        nc.sync.dma_start(out=gates[2][:], in_=gate2)
+
+        xw_u = xw[:].bitcast(U32)
+        tok_words = []
+        tok_scales = []
+
+        def gather(offsets, n, pool, word_tag, scale_tag, bufs):
+            scales = pool.tile([P, n], U8, name="tok_scales", tag=scale_tag, bufs=bufs, align_bytes=64)
+            nc.vector.tensor_copy(scales[:], xs[:].indirect(offsets))
+            words = pool.tile([P, n], U32, name="tok_words", tag=word_tag, bufs=bufs, align_bytes=64)
+            nc.vector.tensor_copy(words[:], xw_u.indirect(offsets))
+            for j in range(n // G):
+                tok_words.append(words[:, j * G : (j + 1) * G])
+                tok_scales.append(scales[:, j * G : (j + 1) * G])
+
+        gather(list1[:, 0:16], G, ring, "tw", "ts", 2)
+        gather(list1[:, 16:32], G, ring, "tw", "ts", 2)
+        experts = [(0, 0), (1, 1), (2, 2), (3, 3), (0, 1), (2, 3)]
+
+        relu = {}
+        codes = {}
+        sums = {}
+        ys = {}
+
+        def hidden(g):
+            for half in range(2):
+                e = experts[g][half]
+                cols = slice(half * P, (half + 1) * P)
+                acc = psum.tile([P, H], F32, name="acc", tag="pa")
+                nc.tensor.matmul_mx(
+                    out=acc[:],
+                    lhsT=tok_words[g][:, cols].bitcast(FP8X4),
+                    lhsT_scale=tok_scales[g][:, cols],
+                    rhs=w1[e].bitcast(FP4X4),
+                    rhs_scale=w1s[:, e, :],
+                    start=True,
+                    stop=True,
+                )
+                r = ring.tile([P, 4, P], F32, name="relu", tag="relu", bufs=4, align_bytes=64)
+                nc.scalar.activation(r[:], acc[:].rearrange("p (m t) -> p t m", t=4), ACT.Relu)
+                relu[g, half] = r
+
+        def turn(g):
+            hb = ring.tile([P, G, 4], BF16, name="hb", tag="hb" if g else "hb0", bufs=3 if g else 1, align_bytes=64)
+            for half in range(2):
+                tp = psum.tile([P, 4, P], F32, name="tp", tag="pt")
+                for t in range(4):
+                    nc.tensor.transpose(tp[:, t, :], relu[g, half][:, t, :], ident[:])
+                nc.scalar.activation(
+                    hb[:, half * P : (half + 1) * P, :], tp[:].rearrange("p t s -> p s t"), ACT.Square
+                )
+            hq = ring.tile([P, G], U32, name="hq", tag="hq", align_bytes=64)
+            hs = ring.tile([P, G], U8, name="hs", tag="hs" if g else "hs0", bufs=3 if g else 1, align_bytes=64)
+            nc.vector.quantize_mx(out=hq[:].bitcast(FP8X4), scales=hs[:], in_=hb[:].rearrange("p s t -> p (s t)"))
+            codes[g] = (hq, hs)
+
+        def project(g):
+            hq, hs = codes[g]
+            ea, eb = experts[g]
+            spans = [(ea, slice(0, G))] if ea == eb else [(ea, slice(0, P)), (eb, slice(P, G))]
+            for pair in range(2):
+                bank = psum.tile([P, 2, G], F32, name="bank", tag="py", bufs=4)
+                for j in range(2):
+                    r = 2 * pair + j
+                    for e, cols in spans:
+                        nc.tensor.matmul_mx(
+                            out=bank[:, j, cols],
+                            lhsT=w2[e][:, 2 * P * r : 2 * P * (r + 1)].bitcast(FP4X4),
+                            lhsT_scale=w2s[:, e, P * r : P * (r + 1)],
+                            rhs=hq[:, cols].bitcast(FP8X4),
+                            rhs_scale=hs[:, cols],
+                            start=True,
+                            stop=True,
+                        )
+                    sums[g, r] = bank[:, j, :]
+
+        def place_first(g, r):
+            y = keep.tile([P, G], F32, name="y_%d_%d" % (g, r), align_bytes=64)
+            nc.scalar.copy(y[:], sums[g, r])
+            nc.vector.tensor_tensor(
+                first[r][:].indirect(list1[:, 16 * g : 16 * (g + 1)]),
+                y[:],
+                gates[g // 2][:, (g % 2) * G : (g % 2 + 1) * G],
+                ALU.mult,
+            )
+
+        def copy_second(g, r):
+            if g == 4:
+                ys[r] = keep.tile([P, 2 * G], F32, name="z_%d" % r, align_bytes=64)
+            nc.scalar.copy(ys[r][:, (g - 4) * G : (g - 3) * G], sums[g, r])
+
+        def place_second(r):
+            nc.vector.tensor_tensor(second[r % 2][:].indirect(list2[:]), ys[r][:], gates[2][:], ALU.mult)
+
+        def add_on_tensor(r):
+            for c in range(2):
+                turned = psum.tile([P, 4, P], F32, name="turned", tag="pa")
+                for b in range(4):
+                    cols = slice((4 * c + b) * P, (4 * c + b + 1) * P)
+                    nc.tensor.matmul(turned[:, b, :], first[r][:, cols], ident[:], start=True, stop=False, is_transpose=True)
+                    nc.tensor.matmul(turned[:, b, :], second[r % 2][:, cols], ident[:], start=False, stop=True, is_transpose=True)
+                mid = ring.tile([P, 4, P], F32, name="mid", tag="relu", bufs=4, align_bytes=64)
+                nc.scalar.copy(mid[:], turned[:])
+                back = psum.tile([P, 4, P], F32, name="back", tag="pt")
+                for b in range(4):
+                    nc.tensor.transpose(back[:, b, :], mid[:, b, :], ident[:])
+                res = ring.tile([P, 4 * P], F32, name="res", tag="res", bufs=4, align_bytes=64)
+                nc.scalar.copy(res[:], back[:].rearrange("p b t -> p (b t)"))
+                nc.sync.dma_start(out=out[P * r : P * (r + 1), 4 * P * c : 4 * P * (c + 1)], in_=res[:])
+
+        def add_on_vector(r):
+            for c in range(2):
+                cols = slice(4 * P * c, 4 * P * (c + 1))
+                res = ring.tile([P, 4 * P], F32, name="res", tag="res", bufs=4, align_bytes=64)
+                nc.vector.tensor_tensor(res[:], first[r][:, cols], second[r % 2][:, cols], ALU.add)
+                nc.sync.dma_start(out=out[P * r : P * (r + 1), cols], in_=res[:])
+
+        hidden(0)
+        gather(list1[:, 32:64], 2 * G, ring, "tw", "ts", 2)
+        turn(0)
+        hidden(1)
+        project(0)
+        gather(list2[:], 2 * G, ring, "hb0", "hs0", 1)
+        place_first(0, 0)
+        turn(1)
+        place_first(0, 1)
+        place_first(0, 2)
+        hidden(2)
+        turn(2)
+        place_first(0, 3)
+        for g in range(1, 4):
+            project(g)
+            place_first(g, 0)
+            hidden(g + 2)
+            place_first(g, 1)
+            turn(g + 2)
+            place_first(g, 2)
+            place_first(g, 3)
+        for g in (4, 5):
+            project(g)
+            for r in range(RB):
+                copy_second(g, r)
+        for r in range(RB):
+            place_second(r)
+            if r < RB - 1:
+                add_on_tensor(r)
+            else:
+                add_on_vector(r)

@@ -1,7 +1,6 @@
 from contextlib import ExitStack
 
 import concourse.mybir as mybir
-from concourse.masks import make_identity
 
 K, T, E, C, D, H, N = 512, 1024, 4, 256, 128, 512, 512
 FLOPS = 2 * (E * C + E * D) * (K * H + H * N)
@@ -34,31 +33,34 @@ def tile_moe_ada_mlp_relu2_kernel(
 
         list1 = lists.tile([P, E * C // 16], U16, name="list1")
         list2 = lists.tile([P, E * D // 16], U16, name="list2")
-        xw = keep.tile([P, T], I32, name="xw", align_bytes=64)
         xs = keep.tile([P, T], U8, name="xs", align_bytes=64)
         w1s = keep.tile([P, E, H], U8, name="w1s", align_bytes=64)
-        w2s = keep.tile([P, E, N], U8, name="w2s", align_bytes=64)
         w1_head = keep.tile([P, 2 * H], U8, name="w1_head", align_bytes=64)
         ident = keep.tile([P, P], F32, name="ident", align_bytes=64)
         first = [keep.tile([P, T], F32, name="first_%d" % r, align_bytes=64) for r in range(RB)]
         second = [keep.tile([P, T], F32, name="second_%d" % i, align_bytes=64) for i in range(2)]
 
-        nc.vector.memset(xs[:].bitcast(I32), 0)
-        nc.vector.memset(w1s[:].bitcast(I32), 0)
-        nc.vector.memset(w2s[:].bitcast(I32), 0)
+        zeros = keep.tile([P, P], F32, name="zeros", tag="x", align_bytes=64)
+        nc.gpsimd.memset(zeros[:], 0.0)
+        nc.gpsimd.memset(xs[:].bitcast(I32), 0)
         with tc.tile_pool(name="scratch", bufs=1) as scratch:
             eye = scratch.tile([P, P], F32, name="eye", align_bytes=64)
-            make_identity(nc, eye[:])
+            nc.gpsimd.affine_select(
+                out=eye[:], in_=zeros[:], compare_op=ALU.not_equal, fill=1.0, base=0, pattern=[[-1, P]], channel_multiplier=1
+            )
             nc.scalar.activation(ident[:], eye[:], ACT.Copy)
+        xw = keep.tile([P, T], I32, name="xw", tag="x", align_bytes=64)
+        nc.gpsimd.memset(w1s[:].bitcast(I32), 0)
         nc.vector.memset(second[0][:], 0.0)
-        nc.gpsimd.memset(second[1][:], 0.0)
+        nc.vector.memset(second[1][:], 0.0)
         late = ctx.enter_context(tc.tile_pool(name="late", bufs=1))
+        w2s = late.tile([P, E, N], U8, name="w2s", align_bytes=64)
+        nc.gpsimd.memset(w2s[:].bitcast(I32), 0)
         w1_rest = late.tile([P, 3, 2 * H], U8, name="w1_rest", align_bytes=64)
-        w2_head = late.tile([P, 2 * N], U8, name="w2_head", align_bytes=64)
-        w2_rest = late.tile([P, 3, 2 * N], U8, name="w2_rest", align_bytes=64)
-        gates = [late.tile([P, 2 * G], F32, name="gate_%d" % i, align_bytes=64) for i in range(3)]
+        w2_head = late.tile([P, 2, 2 * N], U8, name="w2_head", align_bytes=64)
+        gate_head = late.tile([P, 2 * G], F32, name="gate_head", align_bytes=64)
         w1 = [w1_head[:]] + [w1_rest[:, e, :] for e in range(3)]
-        w2 = [w2_head[:]] + [w2_rest[:, e, :] for e in range(3)]
+        w2 = [w2_head[:, e, :] for e in range(2)]
 
         def load_scales(plane, rows):
             for r in range(4):
@@ -71,46 +73,42 @@ def tile_moe_ada_mlp_relu2_kernel(
             )
 
         nc.sync.dma_start(list1[:], offs)
-        nc.sync.dma_start(out=xw[:], in_=x_words.rearrange("s p t d -> p (s t d)").bitcast(I32))
-        nc.sync.dma_start(out=w1_head[:].bitcast(I32), in_=w1_words[0, 0].bitcast(I32))
         nc.sync.dma_start(list2[:], offs2)
+        nc.sync.dma_start(out=w1_head[:].bitcast(I32), in_=w1_words[0, 0].bitcast(I32))
         load_scales(xs[:].bitcast(I32), x_scales.rearrange("s (q r) t -> r q (s t)", r=4).bitcast(I32))
+        nc.sync.dma_start(out=xw[:], in_=x_words.rearrange("s p t d -> p (s t d)").bitcast(I32))
         load_scales(w1s[:].bitcast(I32), w1_scales.rearrange("e s (q r) i -> r q (e s) i", r=4).bitcast(I32))
         load_words(w1_rest, w1_words, 1, 4)
+        load_words(w2_head, w2_words, 0, 2)
+        nc.sync.dma_start(out=gate_head[:], in_=gate1[:, 0 : 2 * G])
         load_scales(w2s[:].bitcast(I32), w2_scales.rearrange("e s (q r) i -> r q (e s) i", r=4).bitcast(I32))
-        nc.sync.dma_start(out=w2_head[:].bitcast(I32), in_=w2_words[0, 0].bitcast(I32))
-        nc.sync.dma_start(out=gates[0][:], in_=gate1[:, 0 : 2 * G])
-        load_words(w2_rest, w2_words, 1, 4)
-        nc.sync.dma_start(out=gates[1][:], in_=gate1[:, 2 * G : 4 * G])
-        nc.sync.dma_start(out=gates[2][:], in_=gate2)
 
         xw_u = xw[:].bitcast(U32)
         tok_words = []
         tok_scales = []
 
-        def gather(offsets, n, pool, word_tag, scale_tag, bufs):
-            scales = pool.tile([P, n], U8, name="tok_scales", tag=scale_tag, bufs=bufs, align_bytes=64)
-            nc.vector.tensor_copy(scales[:], xs[:].indirect(offsets))
-            words = pool.tile([P, n], U32, name="tok_words", tag=word_tag, bufs=bufs, align_bytes=64)
-            nc.vector.tensor_copy(words[:], xw_u.indirect(offsets))
-            for j in range(n // G):
-                tok_words.append(words[:, j * G : (j + 1) * G])
-                tok_scales.append(scales[:, j * G : (j + 1) * G])
+        def gather(window, offsets, n, dtype, tag, bufs, into):
+            got = ring.tile([P, n], dtype, name="got", tag=tag, bufs=bufs, align_bytes=64)
+            nc.vector.tensor_copy(got[:], window.indirect(offsets))
+            into.extend(got[:, j * G : (j + 1) * G] for j in range(n // G))
 
-        gather(list1[:, 0:16], G, ring, "tw", "ts", 2)
-        gather(list1[:, 16:32], G, ring, "tw", "ts", 2)
+        gather(xs[:], list1[:, 0:16], G, U8, "ts", 2, tok_scales)
+        gather(xw_u, list1[:, 0:16], G, U32, "tw0", 1, tok_words)
+        gather(xs[:], list1[:, 16:32], G, U8, "ts", 2, tok_scales)
+        gather(xw_u, list1[:, 16:32], G, U32, "tw1", 1, tok_words)
+        gather(xw_u, list1[:, 32:64], 2 * G, U32, "tw2", 1, tok_words)
         experts = [(0, 0), (1, 1), (2, 2), (3, 3), (0, 1), (2, 3)]
 
+        batch_of = [(0,), (1,), (2, 3), (2, 3), (4, 5), (4, 5)]
+        squares = {}
         relu = {}
         codes = {}
-        sums = {}
-        ys = {}
 
-        def hidden(g):
-            for half in range(2):
+        def hidden(g, halves=(0, 1)):
+            for half in halves:
                 e = experts[g][half]
                 cols = slice(half * P, (half + 1) * P)
-                acc = psum.tile([P, H], F32, name="acc", tag="pa")
+                acc = psum.tile([P, H], F32, name="acc", tag="pair")
                 nc.tensor.matmul_mx(
                     out=acc[:],
                     lhsT=tok_words[g][:, cols].bitcast(FP8X4),
@@ -125,69 +123,62 @@ def tile_moe_ada_mlp_relu2_kernel(
                 relu[g, half] = r
 
         def turn(g):
-            hb = ring.tile([P, G, 4], BF16, name="hb", tag="hb" if g else "hb0", bufs=3 if g else 1, align_bytes=64)
+            lead = batch_of[g][0]
+            if g == lead:
+                n = G * len(batch_of[g])
+                tag = "hb%d" % g
+                squares[lead] = ring.tile([P, n, 4], BF16, name="hb", tag=tag, bufs=1, align_bytes=64)
+            hb = squares[lead]
             for half in range(2):
-                tp = psum.tile([P, 4, P], F32, name="tp", tag="pt")
+                tp = psum.tile([P, 4, P], F32, name="tp", tag="pair")
                 for t in range(4):
                     nc.tensor.transpose(tp[:, t, :], relu[g, half][:, t, :], ident[:])
-                nc.scalar.activation(
-                    hb[:, half * P : (half + 1) * P, :], tp[:].rearrange("p t s -> p s t"), ACT.Square
-                )
-            hq = ring.tile([P, G], U32, name="hq", tag="hq", align_bytes=64)
-            hs = ring.tile([P, G], U8, name="hs", tag="hs" if g else "hs0", bufs=3 if g else 1, align_bytes=64)
-            nc.vector.quantize_mx(out=hq[:].bitcast(FP8X4), scales=hs[:], in_=hb[:].rearrange("p s t -> p (s t)"))
-            codes[g] = (hq, hs)
+                at = (g - lead) * G + half * P
+                nc.scalar.activation(hb[:, at : at + P, :], tp[:].rearrange("p t s -> p s t"), ACT.Square)
+            if g == batch_of[g][-1]:
+                n = G * len(batch_of[g])
+                hq = ring.tile([P, n], U32, name="hq", tag="hq%d" % g, bufs=1, align_bytes=64)
+                hs = ring.tile([P, n], U8, name="hs", tag="hs%d" % g, bufs=1, align_bytes=64)
+                nc.vector.quantize_mx(out=hq[:].bitcast(FP8X4), scales=hs[:], in_=hb[:].rearrange("p s t -> p (s t)"))
+                for j, member in enumerate(batch_of[g]):
+                    codes[member] = (hq[:, j * G : (j + 1) * G], hs[:, j * G : (j + 1) * G])
 
-        def project(g):
-            hq, hs = codes[g]
-            ea, eb = experts[g]
-            spans = [(ea, slice(0, G))] if ea == eb else [(ea, slice(0, P)), (eb, slice(P, G))]
-            for pair in range(2):
-                bank = psum.tile([P, 2, G], F32, name="bank", tag="py", bufs=4)
-                for j in range(2):
-                    r = 2 * pair + j
-                    for e, cols in spans:
-                        nc.tensor.matmul_mx(
-                            out=bank[:, j, cols],
-                            lhsT=w2[e][:, 2 * P * r : 2 * P * (r + 1)].bitcast(FP4X4),
-                            lhsT_scale=w2s[:, e, P * r : P * (r + 1)],
-                            rhs=hq[:, cols].bitcast(FP8X4),
-                            rhs_scale=hs[:, cols],
-                            start=True,
-                            stop=True,
-                        )
-                    sums[g, r] = bank[:, j, :]
-
-        def place_first(g, r):
-            y = keep.tile([P, G], F32, name="y_%d_%d" % (g, r), align_bytes=64)
-            nc.scalar.copy(y[:], sums[g, r])
-            nc.vector.tensor_tensor(
-                first[r][:].indirect(list1[:, 16 * g : 16 * (g + 1)]),
-                y[:],
-                gates[g // 2][:, (g % 2) * G : (g % 2 + 1) * G],
-                ALU.mult,
-            )
-
-        def copy_second(g, r):
-            if g == 4:
-                ys[r] = keep.tile([P, 2 * G], F32, name="z_%d" % r, align_bytes=64)
-            nc.scalar.copy(ys[r][:, (g - 4) * G : (g - 3) * G], sums[g, r])
-
-        def place_second(r):
-            nc.vector.tensor_tensor(second[r % 2][:].indirect(list2[:]), ys[r][:], gates[2][:], ALU.mult)
+        def project(batch, r, tag, bufs):
+            n = G * len(batch)
+            bank = psum.tile([P, n], F32, name="bank", tag=tag, bufs=bufs)
+            for j, g in enumerate(batch):
+                hq, hs = codes[g]
+                ea, eb = experts[g]
+                spans = [(ea, 0, G)] if ea == eb else [(ea, 0, P), (eb, P, G)]
+                for e, lo, hi in spans:
+                    nc.tensor.matmul_mx(
+                        out=bank[:, j * G + lo : j * G + hi],
+                        lhsT=w2[e][:, 2 * P * r : 2 * P * (r + 1)].bitcast(FP4X4),
+                        lhsT_scale=w2s[:, e, P * r : P * (r + 1)],
+                        rhs=hq[:, lo:hi].bitcast(FP8X4),
+                        rhs_scale=hs[:, lo:hi],
+                        start=True,
+                        stop=True,
+                    )
+            y = keep.tile([P, n], F32, name="y_%d_%d_%d" % (batch[0], batch[-1], r), align_bytes=64)
+            nc.scalar.copy(y[:], bank[:])
+            return y
 
         def add_on_tensor(r):
+            mids = []
             for c in range(2):
-                turned = psum.tile([P, 4, P], F32, name="turned", tag="pa")
+                turned = psum.tile([P, 4, P], F32, name="turned", tag="sums", bufs=6)
                 for b in range(4):
                     cols = slice((4 * c + b) * P, (4 * c + b + 1) * P)
                     nc.tensor.matmul(turned[:, b, :], first[r][:, cols], ident[:], start=True, stop=False, is_transpose=True)
                     nc.tensor.matmul(turned[:, b, :], second[r % 2][:, cols], ident[:], start=False, stop=True, is_transpose=True)
                 mid = ring.tile([P, 4, P], F32, name="mid", tag="relu", bufs=4, align_bytes=64)
                 nc.scalar.copy(mid[:], turned[:])
-                back = psum.tile([P, 4, P], F32, name="back", tag="pt")
+                mids.append(mid)
+            for c in range(2):
+                back = psum.tile([P, 4, P], F32, name="back", tag="pair")
                 for b in range(4):
-                    nc.tensor.transpose(back[:, b, :], mid[:, b, :], ident[:])
+                    nc.tensor.transpose(back[:, b, :], mids[c][:, b, :], ident[:])
                 res = ring.tile([P, 4 * P], F32, name="res", tag="res", bufs=4, align_bytes=64)
                 nc.scalar.copy(res[:], back[:].rearrange("p b t -> p (b t)"))
                 nc.sync.dma_start(out=out[P * r : P * (r + 1), 4 * P * c : 4 * P * (c + 1)], in_=res[:])
@@ -195,37 +186,51 @@ def tile_moe_ada_mlp_relu2_kernel(
         def add_on_vector(r):
             for c in range(2):
                 cols = slice(4 * P * c, 4 * P * (c + 1))
-                res = ring.tile([P, 4 * P], F32, name="res", tag="res", bufs=4, align_bytes=64)
+                res = ring.tile([P, 4 * P], F32, name="res", tag="last", bufs=2, align_bytes=64)
                 nc.vector.tensor_tensor(res[:], first[r][:, cols], second[r % 2][:, cols], ALU.add)
                 nc.sync.dma_start(out=out[P * r : P * (r + 1), cols], in_=res[:])
 
+        def place_first(batch, r, held=False):
+            y = project(batch, r, "pair", 2) if held else project(batch, r, "sums", 6)
+            gate = (gate_head if batch[0] < 2 else gate_rest)[:, (batch[0] % 2) * G : (batch[-1] % 2 + 1) * G]
+            offsets = list1[:, 16 * batch[0] : 16 * (batch[-1] + 1)]
+            nc.vector.tensor_tensor(first[r][:].indirect(offsets), y[:], gate, ALU.mult)
+
         hidden(0)
-        gather(list1[:, 32:64], 2 * G, ring, "tw", "ts", 2)
+        gather(xs[:], list1[:, 32:64], 2 * G, U8, "ts", 2, tok_scales)
+        gather(xs[:], list2[:], 2 * G, U8, "tw0", 1, tok_scales)
         turn(0)
-        hidden(1)
-        project(0)
-        gather(list2[:], 2 * G, ring, "hb0", "hs0", 1)
-        place_first(0, 0)
+        gather(xw_u, list2[:], 2 * G, U32, "hb0", 1, tok_words)
+        gate_rest = keep.tile([P, 4 * G], F32, name="gate_rest", tag="x", align_bytes=64)
+        nc.sync.dma_start(out=gate_rest[:, 0 : 2 * G], in_=gate1[:, 2 * G : 4 * G])
+        nc.sync.dma_start(out=gate_rest[:, 2 * G : 4 * G], in_=gate2)
+        hidden(1, (0,))
+        place_first((0,), 0, held=True)
+        hidden(1, (1,))
+        w2_rest = ring.tile([P, 2, 2 * N], U8, name="w2_rest", tag="tw1", bufs=1, align_bytes=64)
+        load_words(w2_rest, w2_words, 2, 4)
+        w2.extend(w2_rest[:, e, :] for e in range(2))
         turn(1)
-        place_first(0, 1)
-        place_first(0, 2)
+        place_first((0,), 1, held=True)
+        place_first((0, 1), 2)
         hidden(2)
+        place_first((1,), 0)
         turn(2)
-        place_first(0, 3)
-        for g in range(1, 4):
-            project(g)
-            place_first(g, 0)
-            hidden(g + 2)
-            place_first(g, 1)
-            turn(g + 2)
-            place_first(g, 2)
-            place_first(g, 3)
-        for g in (4, 5):
-            project(g)
-            for r in range(RB):
-                copy_second(g, r)
+        place_first((1,), 1)
+        hidden(3)
+        turn(3)
+        place_first((0, 1), 3, held=True)
+        place_first((2, 3), 0)
+        hidden(4)
+        turn(4)
+        place_first((2, 3), 1)
+        hidden(5)
+        turn(5)
+        place_first((2, 3), 2, held=True)
+        place_first((2, 3), 3)
+        zs = [project((4, 5), r, "sums", 6) for r in range(RB)]
         for r in range(RB):
-            place_second(r)
+            nc.vector.tensor_tensor(second[r % 2][:].indirect(list2[:]), zs[r][:], gate_rest[:, 2 * G :], ALU.mult)
             if r < RB - 1:
                 add_on_tensor(r)
             else:

@@ -95,8 +95,7 @@ def tile_moe_ada_mlp_relu2_kernel(
         gather(xs[:], list1[:, 0:16], G, U8, "ts", 2, tok_scales)
         gather(xw_u, list1[:, 0:16], G, U32, "tw0", 1, tok_words)
         gather(xs[:], list1[:, 16:32], G, U8, "ts", 2, tok_scales)
-        gather(xw_u, list1[:, 16:32], G, U32, "tw1", 1, tok_words)
-        gather(xw_u, list1[:, 32:64], 2 * G, U32, "tw2", 1, tok_words)
+        gather(xw_u, list1[:, 16:64], 3 * G, U32, "tw1", 1, tok_words)
         experts = [(0, 0), (1, 1), (2, 2), (3, 3), (0, 1), (2, 3)]
 
         batch_of = [(0,), (1,), (2, 3), (2, 3), (4, 5), (4, 5)]
@@ -181,14 +180,13 @@ def tile_moe_ada_mlp_relu2_kernel(
                     nc.tensor.transpose(back[:, b, :], mids[c][:, b, :], ident[:])
                 res = ring.tile([P, 4 * P], F32, name="res", tag="res", bufs=4, align_bytes=64)
                 nc.scalar.copy(res[:], back[:].rearrange("p b t -> p (b t)"))
-                nc.sync.dma_start(out=out[P * r : P * (r + 1), 4 * P * c : 4 * P * (c + 1)], in_=res[:])
+                nc.scalar.dma_start(out=out[P * r : P * (r + 1), 4 * P * c : 4 * P * (c + 1)], in_=res[:])
 
         def add_on_vector(r):
-            for c in range(2):
-                cols = slice(4 * P * c, 4 * P * (c + 1))
-                res = ring.tile([P, 4 * P], F32, name="res", tag="last", bufs=2, align_bytes=64)
-                nc.vector.tensor_tensor(res[:], first[r][:, cols], second[r % 2][:, cols], ALU.add)
-                nc.sync.dma_start(out=out[P * r : P * (r + 1), cols], in_=res[:])
+            for lo, hi, queue in ((0, 512, nc.sync), (512, 896, nc.sync), (896, 1024, nc.sync)):
+                res = ring.tile([P, hi - lo], F32, name="res", tag="last", bufs=3, align_bytes=64)
+                nc.vector.tensor_tensor(res[:], first[r][:, lo:hi], second[r % 2][:, lo:hi], ALU.add)
+                queue.dma_start(out=out[P * r : P * (r + 1), lo:hi], in_=res[:])
 
         def place_first(batch, r, held=False):
             y = project(batch, r, "pair", 2) if held else project(batch, r, "sums", 6)
@@ -207,10 +205,10 @@ def tile_moe_ada_mlp_relu2_kernel(
         hidden(1, (0,))
         place_first((0,), 0, held=True)
         hidden(1, (1,))
-        w2_rest = ring.tile([P, 2, 2 * N], U8, name="w2_rest", tag="tw1", bufs=1, align_bytes=64)
+        turn(1)
+        w2_rest = ring.tile([P, 2, 2 * N], U8, name="w2_rest", tag="hb1", bufs=1, align_bytes=64)
         load_words(w2_rest, w2_words, 2, 4)
         w2.extend(w2_rest[:, e, :] for e in range(2))
-        turn(1)
         place_first((0,), 1, held=True)
         place_first((0, 1), 2)
         hidden(2)
@@ -227,11 +225,12 @@ def tile_moe_ada_mlp_relu2_kernel(
         hidden(5)
         turn(5)
         place_first((2, 3), 2, held=True)
-        place_first((2, 3), 3)
         zs = [project((4, 5), r, "sums", 6) for r in range(RB)]
         for r in range(RB):
             nc.vector.tensor_tensor(second[r % 2][:].indirect(list2[:]), zs[r][:], gate_rest[:, 2 * G :], ALU.mult)
             if r < RB - 1:
                 add_on_tensor(r)
+                if r == 0:
+                    place_first((2, 3), 3, held=True)
             else:
                 add_on_vector(r)

@@ -17,8 +17,16 @@ ACT = mybir.ActivationFunctionType
 ALU = mybir.AluOpType
 
 P = 128
+PACK = 4
 G = 256
-RB = N // P
+GROUP_COLS = G // 16
+ROWS = N // P
+BANK = 512
+PAIR_BANKS, SUM_BANKS = 2, 6
+STAGES = 4
+EXPERTS = ((0, 0), (1, 1), (2, 2), (3, 3), (0, 1), (2, 3))
+BATCH = ((0,), (1,), (2, 3), (2, 3), (4, 5), (4, 5))
+LAST_PIECES = ((0, 512), (512, 896), (896, 1024))
 
 
 def tile_moe_ada_mlp_relu2_kernel(
@@ -28,16 +36,17 @@ def tile_moe_ada_mlp_relu2_kernel(
     with ExitStack() as ctx:
         lists = ctx.enter_context(tc.tile_pool(name="lists", bufs=1))
         keep = ctx.enter_context(tc.tile_pool(name="keep", bufs=1))
-        ring = ctx.enter_context(tc.tile_pool(name="ring", bufs=3))
-        psum = ctx.enter_context(tc.psum_pool(name="psum", bufs=2))
+        ring = ctx.enter_context(tc.tile_pool(name="ring", bufs=1))
+        psum = ctx.enter_context(tc.psum_pool(name="psum", bufs=PAIR_BANKS))
 
         list1 = lists.tile([P, E * C // 16], U16, name="list1")
         list2 = lists.tile([P, E * D // 16], U16, name="list2")
         xs = keep.tile([P, T], U8, name="xs", align_bytes=64)
         w1s = keep.tile([P, E, H], U8, name="w1s", align_bytes=64)
+        w2s = keep.tile([P, E, N], U8, name="w2s", align_bytes=64)
         w1_head = keep.tile([P, 2 * H], U8, name="w1_head", align_bytes=64)
         ident = keep.tile([P, P], F32, name="ident", align_bytes=64)
-        first = [keep.tile([P, T], F32, name="first_%d" % r, align_bytes=64) for r in range(RB)]
+        first = [keep.tile([P, T], F32, name="first_%d" % r, align_bytes=64) for r in range(ROWS)]
         second = [keep.tile([P, T], F32, name="second_%d" % i, align_bytes=64) for i in range(2)]
 
         zeros = keep.tile([P, P], F32, name="zeros", tag="x", align_bytes=64)
@@ -46,66 +55,70 @@ def tile_moe_ada_mlp_relu2_kernel(
         with tc.tile_pool(name="scratch", bufs=1) as scratch:
             eye = scratch.tile([P, P], F32, name="eye", align_bytes=64)
             nc.gpsimd.affine_select(
-                out=eye[:], in_=zeros[:], compare_op=ALU.not_equal, fill=1.0, base=0, pattern=[[-1, P]], channel_multiplier=1
+                out=eye[:],
+                in_=zeros[:],
+                compare_op=ALU.not_equal,
+                fill=1.0,
+                base=0,
+                pattern=[[-1, P]],
+                channel_multiplier=1,
             )
             nc.scalar.activation(ident[:], eye[:], ACT.Copy)
         xw = keep.tile([P, T], I32, name="xw", tag="x", align_bytes=64)
         nc.gpsimd.memset(w1s[:].bitcast(I32), 0)
-        nc.vector.memset(second[0][:], 0.0)
-        nc.vector.memset(second[1][:], 0.0)
-        late = ctx.enter_context(tc.tile_pool(name="late", bufs=1))
-        w2s = late.tile([P, E, N], U8, name="w2s", align_bytes=64)
         nc.gpsimd.memset(w2s[:].bitcast(I32), 0)
-        w1_rest = late.tile([P, 3, 2 * H], U8, name="w1_rest", align_bytes=64)
+        for window in second:
+            nc.scalar.activation(
+                window[:].rearrange("p (b t) -> p b t", t=P),
+                ident[:].unsqueeze(1).to_broadcast([P, T // P, P]),
+                ACT.Copy,
+                scale=0.0,
+            )
+        late = ctx.enter_context(tc.tile_pool(name="late", bufs=1))
+        w1_rest = late.tile([P, E - 1, 2 * H], U8, name="w1_rest", align_bytes=64)
         w2_head = late.tile([P, 2, 2 * N], U8, name="w2_head", align_bytes=64)
         gate_head = late.tile([P, 2 * G], F32, name="gate_head", align_bytes=64)
-        w1 = [w1_head[:]] + [w1_rest[:, e, :] for e in range(3)]
+        w1 = [w1_head[:]] + [w1_rest[:, e, :] for e in range(E - 1)]
         w2 = [w2_head[:, e, :] for e in range(2)]
 
-        def load_scales(plane, rows):
+        def load_scales(tile, blocks):
             for r in range(4):
-                nc.sync.dma_start(out=plane[r:P:32], in_=rows[r])
+                nc.sync.dma_start(out=tile[:].bitcast(I32)[r:P:32], in_=blocks.bitcast(I32)[r])
 
-        def load_words(tile, words, a, b):
+        def load_words(tile, words, e0, e1):
             nc.sync.dma_start(
                 out=tile[:].bitcast(I32),
-                in_=words[a:b].rearrange("e s p b -> p (e s) b").bitcast(I32),
+                in_=words[e0:e1].rearrange("e s p b -> p (e s) b").bitcast(I32),
             )
 
         nc.sync.dma_start(list1[:], offs)
         nc.sync.dma_start(list2[:], offs2)
         nc.sync.dma_start(out=w1_head[:].bitcast(I32), in_=w1_words[0, 0].bitcast(I32))
-        load_scales(xs[:].bitcast(I32), x_scales.rearrange("s (q r) t -> r q (s t)", r=4).bitcast(I32))
+        load_scales(xs, x_scales.rearrange("s (q r) t -> r q (s t)", r=4))
         nc.sync.dma_start(out=xw[:], in_=x_words.rearrange("s p t d -> p (s t d)").bitcast(I32))
-        load_scales(w1s[:].bitcast(I32), w1_scales.rearrange("e s (q r) i -> r q (e s) i", r=4).bitcast(I32))
-        load_words(w1_rest, w1_words, 1, 4)
+        load_scales(w1s, w1_scales.rearrange("e s (q r) i -> r q (e s) i", r=4))
+        load_scales(w2s, w2_scales.rearrange("e s (q r) n -> r q (e s) n", r=4))
+        load_words(w1_rest, w1_words, 1, E)
         load_words(w2_head, w2_words, 0, 2)
         nc.sync.dma_start(out=gate_head[:], in_=gate1[:, 0 : 2 * G])
-        load_scales(w2s[:].bitcast(I32), w2_scales.rearrange("e s (q r) i -> r q (e s) i", r=4).bitcast(I32))
 
-        xw_u = xw[:].bitcast(U32)
         tok_words = []
         tok_scales = []
-
-        def gather(window, offsets, n, dtype, tag, bufs, into):
-            got = ring.tile([P, n], dtype, name="got", tag=tag, bufs=bufs, align_bytes=64)
-            nc.vector.tensor_copy(got[:], window.indirect(offsets))
-            into.extend(got[:, j * G : (j + 1) * G] for j in range(n // G))
-
-        gather(xs[:], list1[:, 0:16], G, U8, "ts", 2, tok_scales)
-        gather(xw_u, list1[:, 0:16], G, U32, "tw0", 1, tok_words)
-        gather(xs[:], list1[:, 16:32], G, U8, "ts", 2, tok_scales)
-        gather(xw_u, list1[:, 16:64], 3 * G, U32, "tw1", 1, tok_words)
-        experts = [(0, 0), (1, 1), (2, 2), (3, 3), (0, 1), (2, 3)]
-
-        batch_of = [(0,), (1,), (2, 3), (2, 3), (4, 5), (4, 5)]
-        squares = {}
         relu = {}
+        squares = {}
         codes = {}
 
-        def hidden(g, halves=(0, 1)):
-            for half in halves:
-                e = experts[g][half]
+        def first_offsets(g0, g1):
+            return list1[:, GROUP_COLS * g0 : GROUP_COLS * g1]
+
+        def gather(window, offsets, groups, dtype, tag, bufs, into):
+            got = ring.tile([P, groups * G], dtype, name="got", tag=tag, bufs=bufs, align_bytes=64)
+            nc.vector.tensor_copy(got[:], window.indirect(offsets))
+            into.extend(got[:, j * G : (j + 1) * G] for j in range(groups))
+
+        def hidden(g):
+            for half in range(2):
+                e = EXPERTS[g][half]
                 cols = slice(half * P, (half + 1) * P)
                 acc = psum.tile([P, H], F32, name="acc", tag="pair")
                 nc.tensor.matmul_mx(
@@ -117,37 +130,35 @@ def tile_moe_ada_mlp_relu2_kernel(
                     start=True,
                     stop=True,
                 )
-                r = ring.tile([P, 4, P], F32, name="relu", tag="relu", bufs=4, align_bytes=64)
-                nc.scalar.activation(r[:], acc[:].rearrange("p (m t) -> p t m", t=4), ACT.Relu)
-                relu[g, half] = r
+                pos = ring.tile([P, PACK, P], F32, name="pos", tag="stage", bufs=STAGES, align_bytes=64)
+                nc.scalar.activation(pos[:], acc[:].rearrange("p (m t) -> p t m", t=PACK), ACT.Relu)
+                relu[g, half] = pos
 
         def turn(g):
-            lead = batch_of[g][0]
-            if g == lead:
-                n = G * len(batch_of[g])
-                tag = "hb%d" % g
-                squares[lead] = ring.tile([P, n, 4], BF16, name="hb", tag=tag, bufs=1, align_bytes=64)
-            hb = squares[lead]
+            batch = BATCH[g]
+            slots = G * len(batch)
+            if g == batch[0]:
+                squares[g] = ring.tile([P, slots, PACK], BF16, name="hb", tag="hb%d" % g, align_bytes=64)
+            hb = squares[batch[0]]
             for half in range(2):
-                tp = psum.tile([P, 4, P], F32, name="tp", tag="pair")
-                for t in range(4):
-                    nc.tensor.transpose(tp[:, t, :], relu[g, half][:, t, :], ident[:])
-                at = (g - lead) * G + half * P
-                nc.scalar.activation(hb[:, at : at + P, :], tp[:].rearrange("p t s -> p s t"), ACT.Square)
-            if g == batch_of[g][-1]:
-                n = G * len(batch_of[g])
-                hq = ring.tile([P, n], U32, name="hq", tag="hq%d" % g, bufs=1, align_bytes=64)
-                hs = ring.tile([P, n], U8, name="hs", tag="hs%d" % g, bufs=1, align_bytes=64)
+                turned = psum.tile([P, PACK, P], F32, name="turned", tag="pair")
+                for t in range(PACK):
+                    nc.tensor.transpose(turned[:, t, :], relu[g, half][:, t, :], ident[:])
+                at = (g - batch[0]) * G + half * P
+                nc.scalar.activation(hb[:, at : at + P, :], turned[:].rearrange("p t s -> p s t"), ACT.Square)
+            if g == batch[-1]:
+                hq = ring.tile([P, slots], U32, name="hq", tag="hq%d" % g, align_bytes=64)
+                hs = ring.tile([P, slots], U8, name="hs", tag="hs%d" % g, align_bytes=64)
                 nc.vector.quantize_mx(out=hq[:].bitcast(FP8X4), scales=hs[:], in_=hb[:].rearrange("p s t -> p (s t)"))
-                for j, member in enumerate(batch_of[g]):
+                for j, member in enumerate(batch):
                     codes[member] = (hq[:, j * G : (j + 1) * G], hs[:, j * G : (j + 1) * G])
 
-        def project(batch, r, tag, bufs):
-            n = G * len(batch)
-            bank = psum.tile([P, n], F32, name="bank", tag=tag, bufs=bufs)
-            for j, g in enumerate(batch):
+        def project(groups, r, in_pair):
+            tag, bufs = ("pair", PAIR_BANKS) if in_pair else ("sums", SUM_BANKS)
+            bank = psum.tile([P, G * len(groups)], F32, name="bank", tag=tag, bufs=bufs)
+            for j, g in enumerate(groups):
                 hq, hs = codes[g]
-                ea, eb = experts[g]
+                ea, eb = EXPERTS[g]
                 spans = [(ea, 0, G)] if ea == eb else [(ea, 0, P), (eb, P, G)]
                 for e, lo, hi in spans:
                     nc.tensor.matmul_mx(
@@ -159,57 +170,63 @@ def tile_moe_ada_mlp_relu2_kernel(
                         start=True,
                         stop=True,
                     )
-            y = keep.tile([P, n], F32, name="y_%d_%d_%d" % (batch[0], batch[-1], r), align_bytes=64)
+            y = keep.tile([P, G * len(groups)], F32, name="y_%d_%d_%d" % (groups[0], groups[-1], r), align_bytes=64)
             nc.scalar.copy(y[:], bank[:])
             return y
 
-        def add_on_tensor(r):
-            mids = []
-            for c in range(2):
-                turned = psum.tile([P, 4, P], F32, name="turned", tag="sums", bufs=6)
-                for b in range(4):
-                    cols = slice((4 * c + b) * P, (4 * c + b + 1) * P)
-                    nc.tensor.matmul(turned[:, b, :], first[r][:, cols], ident[:], start=True, stop=False, is_transpose=True)
-                    nc.tensor.matmul(turned[:, b, :], second[r % 2][:, cols], ident[:], start=False, stop=True, is_transpose=True)
-                mid = ring.tile([P, 4, P], F32, name="mid", tag="relu", bufs=4, align_bytes=64)
-                nc.scalar.copy(mid[:], turned[:])
-                mids.append(mid)
-            for c in range(2):
-                back = psum.tile([P, 4, P], F32, name="back", tag="pair")
-                for b in range(4):
-                    nc.tensor.transpose(back[:, b, :], mids[c][:, b, :], ident[:])
-                res = ring.tile([P, 4 * P], F32, name="res", tag="res", bufs=4, align_bytes=64)
-                nc.scalar.copy(res[:], back[:].rearrange("p b t -> p (b t)"))
-                nc.scalar.dma_start(out=out[P * r : P * (r + 1), 4 * P * c : 4 * P * (c + 1)], in_=res[:])
-
-        def add_on_vector(r):
-            for lo, hi, queue in ((0, 512, nc.sync), (512, 896, nc.sync), (896, 1024, nc.sync)):
-                res = ring.tile([P, hi - lo], F32, name="res", tag="last", bufs=3, align_bytes=64)
-                nc.vector.tensor_tensor(res[:], first[r][:, lo:hi], second[r % 2][:, lo:hi], ALU.add)
-                queue.dma_start(out=out[P * r : P * (r + 1), lo:hi], in_=res[:])
-
-        def place_first(batch, r, held=False):
-            y = project(batch, r, "pair", 2) if held else project(batch, r, "sums", 6)
-            gate = (gate_head if batch[0] < 2 else gate_rest)[:, (batch[0] % 2) * G : (batch[-1] % 2 + 1) * G]
-            offsets = list1[:, 16 * batch[0] : 16 * (batch[-1] + 1)]
+        def place_first(groups, r, in_pair=False):
+            y = project(groups, r, in_pair)
+            gates = gate_head if groups[0] < 2 else gate_rest
+            gate = gates[:, (groups[0] % 2) * G : (groups[-1] % 2 + 1) * G]
+            offsets = first_offsets(groups[0], groups[-1] + 1)
             nc.vector.tensor_tensor(first[r][:].indirect(offsets), y[:], gate, ALU.mult)
 
+        def add_on_tensor(r):
+            mids = []
+            for c in range(T // BANK):
+                both = psum.tile([P, BANK // P, P], F32, name="both", tag="sums", bufs=SUM_BANKS)
+                for b in range(BANK // P):
+                    cols = slice(BANK * c + P * b, BANK * c + P * (b + 1))
+                    nc.tensor.matmul(both[:, b, :], first[r][:, cols], ident[:], start=True, stop=False, is_transpose=True)
+                    nc.tensor.matmul(both[:, b, :], second[r % 2][:, cols], ident[:], start=False, stop=True, is_transpose=True)
+                mid = ring.tile([P, BANK // P, P], F32, name="mid", tag="stage", bufs=STAGES, align_bytes=64)
+                nc.scalar.copy(mid[:], both[:])
+                mids.append(mid)
+            for c in range(T // BANK):
+                back = psum.tile([P, BANK // P, P], F32, name="back", tag="pair")
+                for b in range(BANK // P):
+                    nc.tensor.transpose(back[:, b, :], mids[c][:, b, :], ident[:])
+                res = ring.tile([P, BANK], F32, name="res", tag="res", bufs=STAGES, align_bytes=64)
+                nc.scalar.copy(res[:], back[:].rearrange("p b t -> p (b t)"))
+                nc.scalar.dma_start(out=out[P * r : P * (r + 1), BANK * c : BANK * (c + 1)], in_=res[:])
+
+        def add_on_vector(r):
+            for lo, hi in LAST_PIECES:
+                res = ring.tile([P, hi - lo], F32, name="res", tag="last", bufs=len(LAST_PIECES), align_bytes=64)
+                nc.vector.tensor_tensor(res[:], first[r][:, lo:hi], second[r % 2][:, lo:hi], ALU.add)
+                nc.sync.dma_start(out=out[P * r : P * (r + 1), lo:hi], in_=res[:])
+
+        xw_u = xw[:].bitcast(U32)
+        gather(xs[:], first_offsets(0, 1), 1, U8, "ts", 2, tok_scales)
+        gather(xw_u, first_offsets(0, 1), 1, U32, "tw0", 1, tok_words)
+        gather(xs[:], first_offsets(1, 2), 1, U8, "ts", 2, tok_scales)
+        gather(xw_u, first_offsets(1, E), E - 1, U32, "tw1", 1, tok_words)
         hidden(0)
-        gather(xs[:], list1[:, 32:64], 2 * G, U8, "ts", 2, tok_scales)
-        gather(xs[:], list2[:], 2 * G, U8, "tw0", 1, tok_scales)
+        gather(xs[:], first_offsets(2, E), 2, U8, "ts", 2, tok_scales)
+        gather(xs[:], list2[:], 2, U8, "tw0", 1, tok_scales)
         turn(0)
-        gather(xw_u, list2[:], 2 * G, U32, "hb0", 1, tok_words)
+        gather(xw_u, list2[:], 2, U32, "hb0", 1, tok_words)
         gate_rest = keep.tile([P, 4 * G], F32, name="gate_rest", tag="x", align_bytes=64)
         nc.sync.dma_start(out=gate_rest[:, 0 : 2 * G], in_=gate1[:, 2 * G : 4 * G])
         nc.sync.dma_start(out=gate_rest[:, 2 * G : 4 * G], in_=gate2)
-        hidden(1, (0,))
-        place_first((0,), 0, held=True)
-        hidden(1, (1,))
+
+        hidden(1)
+        place_first((0,), 0, in_pair=True)
         turn(1)
-        w2_rest = ring.tile([P, 2, 2 * N], U8, name="w2_rest", tag="hb1", bufs=1, align_bytes=64)
-        load_words(w2_rest, w2_words, 2, 4)
+        w2_rest = ring.tile([P, 2, 2 * N], U8, name="w2_rest", tag="hb1", align_bytes=64)
+        load_words(w2_rest, w2_words, 2, E)
         w2.extend(w2_rest[:, e, :] for e in range(2))
-        place_first((0,), 1, held=True)
+        place_first((0,), 1, in_pair=True)
         place_first((0, 1), 2)
         hidden(2)
         place_first((1,), 0)
@@ -217,20 +234,21 @@ def tile_moe_ada_mlp_relu2_kernel(
         place_first((1,), 1)
         hidden(3)
         turn(3)
-        place_first((0, 1), 3, held=True)
+        place_first((0, 1), 3, in_pair=True)
         place_first((2, 3), 0)
         hidden(4)
         turn(4)
         place_first((2, 3), 1)
         hidden(5)
         turn(5)
-        place_first((2, 3), 2, held=True)
-        zs = [project((4, 5), r, "sums", 6) for r in range(RB)]
-        for r in range(RB):
+        place_first((2, 3), 2, in_pair=True)
+
+        zs = [project((4, 5), r, False) for r in range(ROWS)]
+        for r in range(ROWS):
             nc.vector.tensor_tensor(second[r % 2][:].indirect(list2[:]), zs[r][:], gate_rest[:, 2 * G :], ALU.mult)
-            if r < RB - 1:
+            if r < ROWS - 1:
                 add_on_tensor(r)
-                if r == 0:
-                    place_first((2, 3), 3, held=True)
             else:
                 add_on_vector(r)
+            if r == 0:
+                place_first((2, 3), ROWS - 1, in_pair=True)

from contextlib import ExitStack

import concourse.mybir as mybir

K, T, E, C, D, H, N = 512, 1024, 4, 256, 128, 512, 512
FLOPS = 2 * (E * C + E * D) * (K * H + H * N)

F32 = mybir.dt.float32
BF16 = mybir.dt.bfloat16
I32 = mybir.dt.int32
U32 = mybir.dt.uint32
U16 = mybir.dt.uint16
U8 = mybir.dt.uint8
FP8X4 = mybir.dt.float8_e4m3fn_x4
FP4X4 = mybir.dt.float4_e2m1fn_x4
ACT = mybir.ActivationFunctionType
ALU = mybir.AluOpType

P = 128
PACK = 4
G = 256
GROUP_COLS = G // 16
ROWS = N // P
BANK = 512
PAIR_BANKS, SUM_BANKS = 2, 6
STAGES = 4
EXPERTS = ((0, 0), (1, 1), (2, 2), (3, 3), (0, 1), (2, 3))
BATCH = ((0,), (1,), (2, 3), (2, 3), (4, 5), (4, 5))
LAST_PIECES = ((0, 512), (512, 896), (896, 1024))


def tile_moe_ada_mlp_relu2_kernel(
    tc, x_words, x_scales, w1_words, w1_scales, w2_words, w2_scales, gate1, gate2, offs, offs2, out
):
    nc = tc.nc
    with ExitStack() as ctx:
        lists = ctx.enter_context(tc.tile_pool(name="lists", bufs=1))
        keep = ctx.enter_context(tc.tile_pool(name="keep", bufs=1))
        ring = ctx.enter_context(tc.tile_pool(name="ring", bufs=1))
        psum = ctx.enter_context(tc.psum_pool(name="psum", bufs=PAIR_BANKS))

        list1 = lists.tile([P, E * C // 16], U16, name="list1")
        list2 = lists.tile([P, E * D // 16], U16, name="list2")
        xs = keep.tile([P, T], U8, name="xs", align_bytes=64)
        w1s = keep.tile([P, E, H], U8, name="w1s", align_bytes=64)
        w2s = keep.tile([P, E, N], U8, name="w2s", align_bytes=64)
        w1_head = keep.tile([P, 2 * H], U8, name="w1_head", align_bytes=64)
        ident = keep.tile([P, P], F32, name="ident", align_bytes=64)
        first = [keep.tile([P, T], F32, name="first_%d" % r, align_bytes=64) for r in range(ROWS)]
        second = [keep.tile([P, T], F32, name="second_%d" % i, align_bytes=64) for i in range(2)]

        zeros = keep.tile([P, P], F32, name="zeros", tag="x", align_bytes=64)
        nc.gpsimd.memset(zeros[:], 0.0)
        nc.gpsimd.memset(xs[:].bitcast(I32), 0)
        with tc.tile_pool(name="scratch", bufs=1) as scratch:
            eye = scratch.tile([P, P], F32, name="eye", align_bytes=64)
            nc.gpsimd.affine_select(
                out=eye[:],
                in_=zeros[:],
                compare_op=ALU.not_equal,
                fill=1.0,
                base=0,
                pattern=[[-1, P]],
                channel_multiplier=1,
            )
            nc.scalar.activation(ident[:], eye[:], ACT.Copy)
        xw = keep.tile([P, T], I32, name="xw", tag="x", align_bytes=64)
        nc.gpsimd.memset(w1s[:].bitcast(I32), 0)
        nc.gpsimd.memset(w2s[:].bitcast(I32), 0)
        for window in second:
            nc.scalar.activation(
                window[:].rearrange("p (b t) -> p b t", t=P),
                ident[:].unsqueeze(1).to_broadcast([P, T // P, P]),
                ACT.Copy,
                scale=0.0,
            )
        late = ctx.enter_context(tc.tile_pool(name="late", bufs=1))
        w1_rest = late.tile([P, E - 1, 2 * H], U8, name="w1_rest", align_bytes=64)
        w2_head = late.tile([P, 2, 2 * N], U8, name="w2_head", align_bytes=64)
        gate_head = late.tile([P, 2 * G], F32, name="gate_head", align_bytes=64)
        w1 = [w1_head[:]] + [w1_rest[:, e, :] for e in range(E - 1)]
        w2 = [w2_head[:, e, :] for e in range(2)]

        def load_scales(tile, blocks):
            for r in range(4):
                nc.sync.dma_start(out=tile[:].bitcast(I32)[r:P:32], in_=blocks.bitcast(I32)[r])

        def load_words(tile, words, e0, e1):
            nc.sync.dma_start(
                out=tile[:].bitcast(I32),
                in_=words[e0:e1].rearrange("e s p b -> p (e s) b").bitcast(I32),
            )

        nc.sync.dma_start(list1[:], offs)
        nc.sync.dma_start(list2[:], offs2)
        nc.sync.dma_start(out=w1_head[:].bitcast(I32), in_=w1_words[0, 0].bitcast(I32))
        load_scales(xs, x_scales.rearrange("s (q r) t -> r q (s t)", r=4))
        nc.sync.dma_start(out=xw[:], in_=x_words.rearrange("s p t d -> p (s t d)").bitcast(I32))
        load_scales(w1s, w1_scales.rearrange("e s (q r) i -> r q (e s) i", r=4))
        load_scales(w2s, w2_scales.rearrange("e s (q r) n -> r q (e s) n", r=4))
        load_words(w1_rest, w1_words, 1, E)
        load_words(w2_head, w2_words, 0, 2)
        nc.sync.dma_start(out=gate_head[:], in_=gate1[:, 0 : 2 * G])

        tok_words = []
        tok_scales = []
        relu = {}
        squares = {}
        codes = {}

        def first_offsets(g0, g1):
            return list1[:, GROUP_COLS * g0 : GROUP_COLS * g1]

        def gather(window, offsets, groups, dtype, tag, bufs, into):
            got = ring.tile([P, groups * G], dtype, name="got", tag=tag, bufs=bufs, align_bytes=64)
            nc.vector.tensor_copy(got[:], window.indirect(offsets))
            into.extend(got[:, j * G : (j + 1) * G] for j in range(groups))

        def hidden(g):
            for half in range(2):
                e = EXPERTS[g][half]
                cols = slice(half * P, (half + 1) * P)
                acc = psum.tile([P, H], F32, name="acc", tag="pair")
                nc.tensor.matmul_mx(
                    out=acc[:],
                    lhsT=tok_words[g][:, cols].bitcast(FP8X4),
                    lhsT_scale=tok_scales[g][:, cols],
                    rhs=w1[e].bitcast(FP4X4),
                    rhs_scale=w1s[:, e, :],
                    start=True,
                    stop=True,
                )
                pos = ring.tile([P, PACK, P], F32, name="pos", tag="stage", bufs=STAGES, align_bytes=64)
                nc.scalar.activation(pos[:], acc[:].rearrange("p (m t) -> p t m", t=PACK), ACT.Relu)
                relu[g, half] = pos

        def turn(g):
            batch = BATCH[g]
            slots = G * len(batch)
            if g == batch[0]:
                squares[g] = ring.tile([P, slots, PACK], BF16, name="hb", tag="hb%d" % g, align_bytes=64)
            hb = squares[batch[0]]
            for half in range(2):
                turned = psum.tile([P, PACK, P], F32, name="turned", tag="pair")
                for t in range(PACK):
                    nc.tensor.transpose(turned[:, t, :], relu[g, half][:, t, :], ident[:])
                at = (g - batch[0]) * G + half * P
                nc.scalar.activation(hb[:, at : at + P, :], turned[:].rearrange("p t s -> p s t"), ACT.Square)
            if g == batch[-1]:
                hq = ring.tile([P, slots], U32, name="hq", tag="hq%d" % g, align_bytes=64)
                hs = ring.tile([P, slots], U8, name="hs", tag="hs%d" % g, align_bytes=64)
                nc.vector.quantize_mx(out=hq[:].bitcast(FP8X4), scales=hs[:], in_=hb[:].rearrange("p s t -> p (s t)"))
                for j, member in enumerate(batch):
                    codes[member] = (hq[:, j * G : (j + 1) * G], hs[:, j * G : (j + 1) * G])

        def project(groups, r, in_pair):
            tag, bufs = ("pair", PAIR_BANKS) if in_pair else ("sums", SUM_BANKS)
            bank = psum.tile([P, G * len(groups)], F32, name="bank", tag=tag, bufs=bufs)
            for j, g in enumerate(groups):
                hq, hs = codes[g]
                ea, eb = EXPERTS[g]
                spans = [(ea, 0, G)] if ea == eb else [(ea, 0, P), (eb, P, G)]
                for e, lo, hi in spans:
                    nc.tensor.matmul_mx(
                        out=bank[:, j * G + lo : j * G + hi],
                        lhsT=w2[e][:, 2 * P * r : 2 * P * (r + 1)].bitcast(FP4X4),
                        lhsT_scale=w2s[:, e, P * r : P * (r + 1)],
                        rhs=hq[:, lo:hi].bitcast(FP8X4),
                        rhs_scale=hs[:, lo:hi],
                        start=True,
                        stop=True,
                    )
            y = keep.tile([P, G * len(groups)], F32, name="y_%d_%d_%d" % (groups[0], groups[-1], r), align_bytes=64)
            nc.scalar.copy(y[:], bank[:])
            return y

        def place_first(groups, r, in_pair=False):
            y = project(groups, r, in_pair)
            gates = gate_head if groups[0] < 2 else gate_rest
            gate = gates[:, (groups[0] % 2) * G : (groups[-1] % 2 + 1) * G]
            offsets = first_offsets(groups[0], groups[-1] + 1)
            nc.vector.tensor_tensor(first[r][:].indirect(offsets), y[:], gate, ALU.mult)

        def add_on_tensor(r):
            mids = []
            for c in range(T // BANK):
                both = psum.tile([P, BANK // P, P], F32, name="both", tag="sums", bufs=SUM_BANKS)
                for b in range(BANK // P):
                    cols = slice(BANK * c + P * b, BANK * c + P * (b + 1))
                    nc.tensor.matmul(both[:, b, :], first[r][:, cols], ident[:], start=True, stop=False, is_transpose=True)
                    nc.tensor.matmul(both[:, b, :], second[r % 2][:, cols], ident[:], start=False, stop=True, is_transpose=True)
                mid = ring.tile([P, BANK // P, P], F32, name="mid", tag="stage", bufs=STAGES, align_bytes=64)
                nc.scalar.copy(mid[:], both[:])
                mids.append(mid)
            for c in range(T // BANK):
                back = psum.tile([P, BANK // P, P], F32, name="back", tag="pair")
                for b in range(BANK // P):
                    nc.tensor.transpose(back[:, b, :], mids[c][:, b, :], ident[:])
                res = ring.tile([P, BANK], F32, name="res", tag="res", bufs=STAGES, align_bytes=64)
                nc.scalar.copy(res[:], back[:].rearrange("p b t -> p (b t)"))
                nc.scalar.dma_start(out=out[P * r : P * (r + 1), BANK * c : BANK * (c + 1)], in_=res[:])

        def add_on_vector(r):
            for lo, hi in LAST_PIECES:
                res = ring.tile([P, hi - lo], F32, name="res", tag="last", bufs=len(LAST_PIECES), align_bytes=64)
                nc.vector.tensor_tensor(res[:], first[r][:, lo:hi], second[r % 2][:, lo:hi], ALU.add)
                nc.sync.dma_start(out=out[P * r : P * (r + 1), lo:hi], in_=res[:])

        xw_u = xw[:].bitcast(U32)
        gather(xs[:], first_offsets(0, 1), 1, U8, "ts", 2, tok_scales)
        gather(xw_u, first_offsets(0, 1), 1, U32, "tw0", 1, tok_words)
        gather(xs[:], first_offsets(1, 2), 1, U8, "ts", 2, tok_scales)
        gather(xw_u, first_offsets(1, E), E - 1, U32, "tw1", 1, tok_words)
        hidden(0)
        gather(xs[:], first_offsets(2, E), 2, U8, "ts", 2, tok_scales)
        gather(xs[:], list2[:], 2, U8, "tw0", 1, tok_scales)
        turn(0)
        gather(xw_u, list2[:], 2, U32, "hb0", 1, tok_words)
        gate_rest = keep.tile([P, 4 * G], F32, name="gate_rest", tag="x", align_bytes=64)
        nc.sync.dma_start(out=gate_rest[:, 0 : 2 * G], in_=gate1[:, 2 * G : 4 * G])
        nc.sync.dma_start(out=gate_rest[:, 2 * G : 4 * G], in_=gate2)

        hidden(1)
        place_first((0,), 0, in_pair=True)
        turn(1)
        w2_rest = ring.tile([P, 2, 2 * N], U8, name="w2_rest", tag="hb1", align_bytes=64)
        load_words(w2_rest, w2_words, 2, E)
        w2.extend(w2_rest[:, e, :] for e in range(2))
        place_first((0,), 1, in_pair=True)
        place_first((0, 1), 2)
        hidden(2)
        place_first((1,), 0)
        turn(2)
        place_first((1,), 1)
        hidden(3)
        turn(3)
        place_first((0, 1), 3, in_pair=True)
        place_first((2, 3), 0)
        hidden(4)
        turn(4)
        place_first((2, 3), 1)
        hidden(5)
        turn(5)
        place_first((2, 3), 2, in_pair=True)

        zs = [project((4, 5), r, False) for r in range(ROWS)]
        for r in range(ROWS):
            nc.vector.tensor_tensor(second[r % 2][:].indirect(list2[:]), zs[r][:], gate_rest[:, 2 * G :], ALU.mult)
            if r < ROWS - 1:
                add_on_tensor(r)
            else:
                add_on_vector(r)
            if r == 0:
                place_first((2, 3), ROWS - 1, in_pair=True)
